import numpy as np, ml_dtypes
CORES = [24,25,26,27,28,29,30,31]
N = 8
BF = ml_dtypes.bfloat16
P, V, C, PH, S, Z, CAP, RO = 2048, 1024, 1024, 2, 4, 4, 128, 3
I = V // PH
def tail(rng, b, top):
    return np.where(np.arange(16)[:, None] >= rng.integers(0, 17, (N, 8, 1, V)), rng.integers(0, top, b.shape), b)
def parts(rng):
    e = rng.choice(np.array([10.0, 14.0, 18.0, 24.0]), (N, 8, 1, 1))
    x = np.minimum((256 * rng.random((N, 8, 16, P)) ** e).astype(np.int64), 255)
    m = rng.integers(0, 256, (N, 8, 16, V)); b = rng.integers(0, P, (N, 8, 16, V))
    return x, m, b, tail(rng, b, P), rng.integers(0, V, (N, 8, 16, C))
def tops(x, l):
    y = np.take_along_axis(x, l[:, :, 0][:, :, None, :], 3)
    for k in range(1, 16): y = np.maximum(y, np.take_along_axis(x, l[:, :, k][:, :, None, :], 3))
    return y
def late(rng, shape):
    return PH * rng.integers(0, I, shape) + 1 + rng.integers(0, PH - 1, shape)
def pack(x, m, b, d, u):
    r = {"mor": x.reshape(N, 128, P).astype(np.float32).astype(BF), "mea": m.reshape(N, 128, V).astype(np.float32).astype(BF)}
    r["bas"] = b.reshape(N, 128, V).astype(np.int32); r["der"] = d.reshape(N, 128, V).astype(np.int32); r["use"] = u.reshape(N, 128, C).astype(np.int32)
    return r
def setup_inputs(rng):
    x, m, b, d, u = parts(rng); h = rng.integers(0, 8, N)
    for q in range(N):
        g = int(h[q]); x[q, g, :, P - 1] = 255; m[q, g] = rng.integers(0, 151, (16, V)); u[q, g] = late(rng, (16, C))
        d[q, g, rng.integers(0, 16, I), PH * np.arange(I)] = P - 1
    near = rng.random((N, 8, 1, V)) < rng.choice(np.array([0.0, 0.2, 0.5, 0.8]), (N, 8, 1, 1)); near[np.arange(N), h] = False
    m = np.where(near, np.clip(tops(x, d) + rng.integers(-24, 25, m.shape), 0, 255), m)
    for q in range(N):
        for g in range(8):
            v = PH * rng.permutation(I)[:3]; u[q, g][:, b[q, g, 15, v] & (C - 1)] = v
    return pack(x, m, b, d, u)
def setup_inputs_corners(rng):
    x, m, b, d, u = parts(rng); x = np.minimum(x, 100); x[..., P - 1] = 255; m = rng.integers(0, 101, m.shape)
    b = rng.integers(0, P - 1, b.shape); d = tail(rng, b, P - 1); u = late(rng, u.shape)
    u = np.where(rng.random((N, 8, 1, C)) < 0.1, np.where(rng.random((N, 8, 1, C)) < 0.5, V - 1, 1), u); top = tops(x, d)
    for q in range(N):
        for g in range(8):
            if q == 3 and g % 2 == 1:
                n = (0, 1, CAP // 2, CAP - 1)[g // 2]; o = PH * np.arange(I); w = PH * rng.permutation(I) + 1
                m[q, g][:, o] = top[q, g][:, o]; m[q, g][:, w[:n]] = top[q, g][:, w[:n]]
                d[q, g, rng.integers(0, 16, I - n), w[n:]] = P - 1; u[q, g] = PH * rng.integers(0, I, (16, C))
                continue
            n = int(rng.choice(np.array([0, 1, CAP - 1, CAP, CAP + 1, I])))
            if q == 0: n = (CAP, CAP + 1, I, CAP - 1, 1, 0, CAP, CAP + 1)[g]
            if q == 1 or q == 2: n = (CAP, 1, CAP - 1, 0)[g % 4]
            if q == 2 and g == 7: n = CAP + 1
            o = PH * rng.permutation(I); nl = min(n, C // 2); lone, fit, ad = o[:nl], o[nl:n], o[n:]
            cols = 2 * rng.permutation(C // 2)[:nl] + q % 2
            b[q, g, 15, lone] = cols + C * rng.integers(0, P // C - 1, nl); u[q, g][:, cols] = lone
            b[q, g, 15, ad] = 2 * rng.integers(0, C // 2, I - n) + 1 - q % 2 + C * rng.integers(0, P // C - 1, I - n)
            bad = np.concatenate([lone, ad]); d[q, g, rng.integers(0, 16, len(bad)), bad] = P - 1
            m[q, g][:, fit] = top[q, g][:, fit]
            if q == 2:
                o = PH * np.arange(I); z = np.add.reduce(np.arange(1, 17)[:, None] * m[q, g][:, o], axis=0) & (Z - 1)
                left = np.ones(P, dtype=bool); left[P - 1] = False; left[S * np.arange(I) + z] = False
                l = d[q, g][:, o + 1]; l = np.where(left[l], l, rng.choice(np.flatnonzero(left), l.shape))
                d[q, g][:, o + 1] = l; m[q, g][:, o + 1] = np.maximum.reduce(x[q, g][:, l], axis=1)
    return pack(x, m, b, d, u)
def setup_inputs_ties(rng):
    x, m, b, d, u = parts(rng); x[:, 1::2] = x[:, 1::2] >> 6
    k = rng.integers(0, 8, (N, 8, 1, V)); m = np.take_along_axis(m[..., :8], k, 3); m[:, 1::2] = m[:, 1::2] >> 6
    b[:, :2] = np.take_along_axis(b[:, :2, :, :8], k[:, :2], 3); d[:, :2] = np.take_along_axis(d[:, :2, :, :8], k[:, :2], 3)
    lane = np.arange(V); a = rng.integers(40, 81, (N, 16, 1)); high = (np.arange(16)[:, None] == 15) & (lane >= V // 2)
    m[:, 6] = np.where(lane % PH == 0, rng.integers(215, 256, (N, 16, V)), a + high); u[:, 6] = late(rng, (N, 16, C))
    u[..., ::2] = u[:, :, np.arange(16) & 3, ::2]
    return pack(x, m, b, d, u)
def setup_inputs_alike(rng):
    x, m, b, d, u = parts(rng)
    d[:, :3] = b[:, :3]; d[:, 1, 0] = (b[:, 1, 0] + 1) % P; d[:, 2, 15] = (b[:, 2, 15] + 1) % P
    b[:, 3, 15] = rng.integers(0, P, (N, 1)); u[:, 4] = rng.integers(0, V, (N, 1, C))
    for q in range(N):
        v = PH * rng.permutation(I)[:I // 4]; u[q, 4][:, b[q, 4, 15, v] & (C - 1)] = v
    b[:, 5] = rng.integers(0, P, (N, 1, V)); d[:, 5] = rng.integers(0, P, (N, 1, V)); u[:, 6] = (V - 1) * rng.integers(0, 2, (N, 16, C))
    for q in range(N):
        v = PH * rng.permutation(I)[:I // 8]; c = b[q, 7, 15, v] & (C - 1); u[q, 7][:, c] = v; u[(q + 1) % N, 7][:, c] = v
    return pack(x, m, b, d, u)
def setup_inputs_spread(rng):
    x = (np.exp2(8 * rng.random((N, 8, 1, P))) * rng.random((N, 8, 16, P)) ** 3).astype(np.int64)
    m = (np.exp2(8 * rng.random((N, 8, 1, V))) * rng.random((N, 8, 16, V))).astype(np.int64)
    e = rng.choice(np.array([1.0, 2.0, 4.0, 8.0]), (3, N, 8, 1, 1))
    b = (P * rng.random((N, 8, 16, V)) ** e[0]).astype(np.int64); c = (P * rng.random((N, 8, 16, V)) ** e[1]).astype(np.int64)
    d = np.where(np.arange(16)[:, None] >= rng.integers(0, 17, (N, 8, 1, V)), c, b); u = (V * rng.random((N, 8, 16, C)) ** e[2]).astype(np.int64)
    return pack(np.clip(x, 0, 255), np.clip(m, 0, 255), np.clip(b, 0, P - 1), np.clip(d, 0, P - 1), np.clip(u, 0, V - 1))
def setup_inputs_ends(rng):
    def bits(p, n): return 255 * (rng.random((N, 8, 16, n)) < p)
    def lists(n, hi):
        k = rng.random((N, 8, 1, n)); a = hi * rng.integers(0, 2, (N, 8, 16, n))
        return np.where(k < 0.25, 0, np.where(k < 0.5, hi, np.where(k < 0.8, a, rng.integers(0, hi + 1, (N, 8, 16, n)))))
    k = rng.random((N, 8, 1, P)); x = np.where(k < 0.6, 0, np.where(k < 0.63, 255, bits(0.06, P)))
    k = rng.random((N, 8, 1, V)); m = np.where(k < 0.25, 0, np.where(k < 0.5, 255, bits(0.5, V)))
    b = lists(V, P - 1); d = np.where(np.arange(16)[:, None] >= rng.integers(0, 17, (N, 8, 1, V)), lists(V, P - 1), b); u = lists(C, V - 1)
    for t in range(RO):
        for c in (97 * t, 97 * t - 1):
            u[..., c & (C - 1)] = np.where(rng.random((N, 8, 16)) < 0.5, (V - 1) * rng.integers(0, 2, (N, 8, 16)), rng.integers(0, V, (N, 8, 16)))
    x[:, ::2, :, 0] = 255 * rng.integers(0, 2, (N, 4, 16)); x[:, ::2, :, P - 1] = 255 * rng.integers(0, 2, (N, 4, 16)); x[:, 1::2, :, 0] = 0; x[:, 1::2, :, P - 1] = 255
    lo, hi = PH - 1 + PH * (PH % 2), V - 1 - PH
    m[:, 1::2, :, :PH - 1] = 0; m[:, 1::2, :, V - PH:V - 1] = 255; m[..., V - 1] = 255
    m[:, 1::2, :, lo] = 0; m[:, 1::2, :, hi] = 0; m[:, ::2, :, lo] = 255; m[:, ::2, :, hi] = 255
    u[:, 1::2, :, 0] = np.where(np.arange(16) % 2 == 0, 0, V - 1); b[:, 1::2, :, 0] = 0; d[:, 1::2, :, 0] = P - 1
    u[..., C - 1] = np.where(np.arange(16) % 2 == 0, hi, lo)
    b[..., lo] = 0; d[..., lo] = P - 1; b[..., hi] = P - 1; d[..., hi] = 0; d[..., V - 1] = 0
    b[:, :, 15, V - 1] = ((C - 1 - 97 * (PH - 1)) & (C - 1)) + P - C
    return pack(x, m, b, d, u)
def check_inputs(d):
    bad = []
    for k, hi in (("mor", 255), ("mea", 255), ("bas", P - 1), ("der", P - 1), ("use", V - 1)):
        a = np.asarray(d[k]).astype(np.float64)
        if not np.all((a >= 0) & (a <= hi) & (a == np.floor(a))): bad.append("range of " + k)
    return bad
def pick(a, ix):
    return np.stack([np.take(a[g], ix[g], axis=1) for g in range(8)])
def model(kap, mv, own, m, b, d, u):
    c = pick(u, kap)
    s = np.add.reduce(np.abs(pick(m, c) - mv[:, :, None, :]), axis=1)
    k = np.minimum.reduce(np.where(c == own, 2 ** 24, s * 2048 + c), axis=1)
    ok = k < 2 ** 24; w = np.where(ok, k & 2047, 0); dm = pick(d, w)
    diff = pick(b, w) != dm; diff[:, 15] = True
    return ok, w, np.argmax(diff, axis=1), dm
def gap(x, l, mv):
    return np.add.reduce(np.abs(np.maximum.reduce(pick(x, l), axis=2) - mv), axis=1)
def reference(mor, mea, bas, der, use):
    x = mor.astype(np.float32).astype(np.int32).reshape(N, 8, 16, P); m = mea.astype(np.float32).astype(np.int32).reshape(N, 8, 16, V)
    b = bas.astype(np.int32).reshape(N, 8, 16, V); d = der.astype(np.int32).reshape(N, 8, 16, V); u = use.astype(np.int32).reshape(N, 8, 16, C)
    row = np.arange(16)[None, :, None]; i = np.arange(I); count = [0] * N
    for t in range(RO):
        v = PH * i + t % PH; todo = []
        for r in range(N):
            mv = m[r][:, :, v]; bv = b[r][:, :, v]; dv = d[r][:, :, v]; kap = (bv[:, 15] + 97 * t) & (C - 1); mar = count[r] & 127
            ok, w, f, dm = model(kap, mv, v, m[r], b[r], d[r], u[r])
            e = np.where(row < f[:, None, :], bv, dm); old = gap(x[r], dv, mv)
            ad = ok & (gap(x[r], e, mv) + mar < old)
            q = (r + 1 + t % (N - 1)) % N
            sel = np.argsort(ad, axis=1, kind="stable")[:, :CAP]
            asks = ~np.take_along_axis(ad, sel, 1); mv2 = pick(mv, sel)
            ok2, w2, f2, dm2 = model(np.take_along_axis(kap, sel, 1), mv2, -1, m[q], b[q], d[q], u[q])
            e2 = np.where(row < f2[:, None, :], pick(bv, sel), dm2)
            ad2 = asks & (gap(x[r], e2, mv2) + mar < np.take_along_axis(old, sel, 1))
            new = np.where(ad[:, None, :], e, dv); got = ad.copy()
            for g in range(8):
                new[g][:, sel[g][ad2[g]]] = e2[g][:, ad2[g]]; got[g, sel[g][ad2[g]]] = True
            todo.append((ad, w, new, got, (np.add.reduce((row + 1) * mv, axis=1) + t) & (Z - 1)))
        for r in range(N):
            ad, w, new, got, z = todo[r]; d[r][:, :, v] = new; count[r] = int(np.count_nonzero(got))
            for g in range(8):
                j = i[ad[g]]; u[r, g, (j + t) & 15, (j + 37 * t) & (C - 1)] = w[g][j] ^ 1
                j = i[got[g]]; x[r, g][:, S * j + z[g][j]] = m[r, g][:, v[j]]
    return {"yd": d.reshape(N, 128, V).astype(np.float32), "yu": u.reshape(N, 128, C).astype(np.float32), "ym": x.reshape(N, 128, P).astype(np.float32).astype(BF)}

@@ -1,0 +1,516 @@
+from concourse.mybir import AluOpType as OP, AxisListType, ActivationFunctionType as AF
+
+S_, P_ = "sbuf", "psum"
+F, B, I, U = "float32", "bfloat16", "int32", "uint16"
+MO, MD, MX = 512, 2560, 4608
+SCRATCH = {}
+
+
+def _buf(names, n, d, where=S_):
+    for x in names.split():
+        SCRATCH[x] = (where, [128, n], d)
+
+
+_buf("b15", 994, I)
+_buf("basi deri usei", 1024, I)
+_buf("meas", 1024, B)
+_buf("morw", 4624, B)
+_buf("usef ydb", 1024, F)
+_buf("tl xr", 2048, F)
+_buf("mvt0 mvt1 got", 640, B)
+_buf("bst0 bst1 gds cq", 640, F)
+_buf("dri0 dri1 nd", 640, I)
+_buf("dro0 dro1 cdo eo", 512, U)
+_buf("rep0 rep1 dm gd", 8192, B)
+_buf("mq0 mq1 mq2", 1024, B)
+_buf("uq0 uq1 uq2 tq0 tq1 tq2", 1024, F)
+_buf("wi wj pi pk zi zt zu", 32, I)
+_buf("kap0 kap1 kap2 wo gu", 32, U)
+_buf("gf zw0 zw1 zc i16 iw", 32, F)
+_buf("cdf eq ks ec dk vr0 vr1 minm", 512, F)
+_buf("um us m8 m8r", 256, F)
+_buf("es rp2 rm zsp dg", 2048, B)
+_buf("dd ee fail cum junk sg neq", 512, B)
+_buf("marg cn thr jp", 1, F)
+_buf("acc sm bj j2", 8, F)
+_buf("sel w2o", 8, U)
+_buf("c2f bs2 gd2 dr2 ks2 ec2 x2 ad2 y2 n2 id1 idb on", 128, F)
+_buf("c2o eo2", 128, U)
+_buf("mv2 ee2 b1 bm tri idh idn wz", 128, B)
+_buf("um2 us2", 64, F)
+_buf("g8", 8, B)
+_buf("la", 1024, F)
+_buf("kin", 528, I)
+_buf("km", 528, B)
+_buf("pK pU pG pD pC pM pX0 pX1", 512, F, P_)
+SEMAPHORES = ["cv", "cs", "cp", "cg"] + ["d%d" % i for i in range(24)] + ["rl%d" % i for i in range(9)] + ["ar%d" % i for i in range(9)]
+BIG = float(2 ** 25)
+ESPLIT = "ssvsssvs"
+DSPLIT = ("ssss", "svss", "svss")
+MSPLIT = ("vvvvvvvv", "ppvvpvvv", "ppvvpvvv")
+FILL = (4, 1, 1, 2)
+
+
+def rank_program(g, core, T, topo):
+    rank = T.rank_of(core)
+    if rank is None:
+        return
+    queue = {"v": g.vector, "s": g.scalar, "p": g.tensor, "g": g, "y": g.sync}
+    clock = {q: {} for q in queue}
+    total, log, nd = {}, {}, [0]
+
+    def X(name, lo=0, hi=None, st=None):
+        hi = SCRATCH[name][1][1] if hi is None else hi
+        return (T[name][:, lo:hi] if st is None else T[name][:, lo:hi:st], name, lo, hi)
+
+    def emit(q, fn, R, W, sem=None, n=1, tot=None):
+        deps = []
+        touch = [(v[1], v[2], v[3], False) for v in R] + [(v[1], v[2], v[3], True) for v in W]
+        for name, lo, hi, w in touch:
+            ps = SCRATCH[name][0] == "psum"
+            for rec in log.get(name, []):
+                if not ps and (rec[1] <= lo or hi <= rec[0]):
+                    continue
+                if not (w or rec[2] or ps):
+                    continue
+                if rec[3] == q and sem is None and rec[7]:
+                    if q == "p" or not (w or rec[2]) or rec[1] <= lo or hi <= rec[0]:
+                        continue
+                deps.append(rec)
+        for rec in sorted(deps, key=lambda r: -r[8]):
+            if clock[q].get(rec[4], 0) < rec[5]:
+                queue[q].wait_ge(T.sem[rec[4]], rec[5])
+                for s, c in rec[6].items():
+                    clock[q][s] = max(clock[q].get(s, 0), c)
+        comp = sem is None
+        s = {"v": "cv", "s": "cs", "p": "cp", "g": "cg"}[q] if comp else sem
+        ins = fn(queue[q])
+        if n:
+            ins.then_inc(T.sem[s], n)
+        total[s] = total.get(s, 0) + n if comp else (tot or n)
+        c = dict(clock[q])
+        c[s] = total[s]
+        nd[0] += 1
+        for name, lo, hi, w in touch:
+            recs = log.setdefault(name, [])
+            if w:
+                recs = [r for r in recs if not (lo <= r[0] and r[1] <= hi)]
+            else:
+                recs = [r for r in recs if not (r[3] == q and comp and r[7] and not r[2] and lo <= r[0] and r[1] <= hi)]
+            recs.append((lo, hi, w, q, s, total[s], c, comp, nd[0]))
+            log[name] = recs
+
+    nsem = [0]
+
+    def dma(q, out, in_, R=(), W=(), sem=None, tot=None):
+        if sem is None:
+            sem = "d%d" % nsem[0]
+            nsem[0] += 1
+        emit(q, lambda e: e.dma_start(out, in_), R, W, sem=sem, n=16, tot=tot or 16)
+
+    def ind(win, off):
+        return (win[0].indirect(off[0]), win, off)
+
+    def rd(*vs):
+        r = []
+        for v in vs:
+            r += [v[1], v[2]] if len(v) == 3 else [v]
+        return r
+
+    def tt(out, a, b, op):
+        emit("v", lambda e: e.tensor_tensor(out[0], a[0], b[0], op), rd(a, b), [out])
+
+    def ts(out, a, s1, op0, s2=None, op1=None):
+        R = rd(a) + ([s1] if isinstance(s1, tuple) else [])
+        k1 = s1[0] if isinstance(s1, tuple) else s1
+        if op1 is None:
+            emit("v", lambda e: e.tensor_scalar(out[0], a[0], k1, None, op0), R, [out])
+        else:
+            emit("v", lambda e: e.tensor_scalar(out[0], a[0], k1, s2, op0, op1), R, [out])
+
+    def cp(out, a):
+        if len(out) == 3:
+            emit("v", lambda e: e.tensor_copy(out[0], a[0]), rd(a) + [out[2]], [out[1]])
+        else:
+            emit("v", lambda e: e.tensor_copy(out[0], a[0]), rd(a), [out])
+
+    def ms(out, val):
+        emit("v", lambda e: e.memset(out[0], val), [], [out])
+
+    def scan(out, d0, d1, init, op0, op1):
+        emit("v", lambda e: e.tensor_tensor_scan(out[0], d0[0], d1[0], init, op0, op1), [d0, d1], [out])
+
+    def act(out, a, func, bias=0.0, scale=1.0, accum=None):
+        R = rd(a) + ([bias] if isinstance(bias, tuple) else [])
+        k = bias[0] if isinstance(bias, tuple) else bias
+        if accum:
+            emit("s", lambda e: e.activation(out[0], a[0], func, bias=k, scale=scale, accum_out=accum[0]), R, [out, accum])
+        else:
+            emit("s", lambda e: e.activation(out[0], a[0], func, bias=k, scale=scale), R, [out])
+
+    def mm(out, l, r, start, stop):
+        emit("p", lambda e: e.matmul(out[0], l[0], r[0], start, stop), [l, r], [out])
+
+    def iota(out, pat, base, cm, flt):
+        emit("g", lambda e: e.iota(out[0], pat, base, cm, allow_small_or_imprecise_dtypes=True) if flt else e.iota(out[0], pat, base, cm), [], [out])
+
+    def asel(b, pat, op, base, cm):
+        emit("g", lambda e: e.affine_select(b[0], b[0], pat, op, 0.0, base, cm), [b], [b])
+
+    cores = T.cores
+
+    def send(src, dst, t, ix):
+        to = cores[(rank - 1 - t) % len(cores)]
+        e = topo.engines(core, to)[:8]
+        m = sum(1 << k for k in e)
+        a = topo.addr(to)
+        out = T[dst][:, 0:1024]
+        emit("g", lambda q: q.remote_dma(out, src[0], T.sem["ar%d" % ix], T.sem["rl%d" % ix], a[1], a[0], m), [src], [], sem="rl%d" % ix, n=0, tot=len(e))
+        log.setdefault(dst, []).append((0, 1024, True, "x", "ar%d" % ix, len(e), {"ar%d" % ix: len(e)}, False, 0))
+        total["ar%d" % ix] = len(e)
+
+    for b in range(16):
+        dma("y" if b % 2 == 0 else "s", T.b15[b::16, 0:994], T.bas[15::16, 2 * b:2 * b + 994], W=[X("b15")] if b == 15 else [], sem="d0", tot=256)
+    nsem[0] = 1
+    dma("y", T.meas[:], T.mea[:], W=[X("meas")])
+    dma("s", T.usei[:], T.use[:], W=[X("usei")])
+    dma("y", T.deri[:], T.der[:], W=[X("deri")])
+    dma("s", T.morw[:, MO:MD], T.mor[:], W=[X("morw", MO, MD)])
+    dma("y", T.basi[:], T.bas[:], W=[X("basi")])
+    dma("y", T.morw[:, MD:MX], T.mor[:], W=[X("morw", MD, MX)])
+
+    def same(b, o, st):
+        asel(b, o + [[-16, 8]] + st, OP.is_ge, 0, 1)
+        asel(b, o + [[16, 8]] + st, OP.is_ge, 15, -1)
+
+    ms(X("rm"), 1.0)
+    ms(X("zsp"), 0.0)
+    ms(X("rm", 0, 2048, 16), 0.0)
+    ms(X("g8"), 2048.0)
+    ms(X("id1"), 1.0)
+    ms(X("idb"), float(2 ** 23 + 1024))
+    ms(X("mvt0", 512, 640), 0.0)
+    ms(X("idh"), 1.0)
+    ms(X("idn"), -1.0)
+    ms(X("minm"), 0.0)
+    ms(X("la"), 1.0)
+    ms(X("minm", 0, 512, 16), BIG)
+    ms(X("m8"), 1.0)
+    ms(X("b1"), 1.0)
+    same(X("g8"), [], [])
+    for n in ("id1", "idb", "idh", "idn"):
+        asel(X(n), [[-1, 128]], OP.is_equal, 0, 1)
+    iota(X("vr0"), [[2, 512]], 0, 0, True)
+    iota(X("pi"), [[0, 32]], 0, 1, False)
+    send(X("meas"), "mq0", 0, 0)
+    asel(X("la"), [[-16, 8], [0, 8], [-1, 16]], OP.is_equal, 0, 1)
+    same(X("m8"), [[0, 32]], [])
+    same(X("b1"), [], [[0, 16]])
+    iota(X("i16"), [[16, 32]], 0, 0, True)
+    iota(X("kin"), [[-1, 528]], 1024, 1, False)
+
+    def kap(t):
+        ts(X("zt"), X("b15", t % 2, 994, 32), 97 * t, OP.add)
+        ts(X("zu"), X("zt"), 1023, OP.bitwise_and)
+        cp(X("kap%d" % t), X("zu"))
+
+    def prep(t):
+        cp(X("cdf"), ind(X("usef") if t else X("usei"), X("kap%d" % t)))
+        cp(X("cdo"), X("cdf"))
+        tt(X("eq"), X("cdf"), X("vr%d" % (t % 2)), OP.is_equal)
+
+    late = []
+
+    def chunk(t, c):
+        sl = X("dm", 1024 * c, 1024 * c + 1024)
+        rep = "rep%d" % (t % 2)
+        src = ind(X("meas"), X("cdo", 64 * c, 64 * c + 64))
+        if MSPLIT[t][c] == "v":
+            tt(sl, src, X(rep, 1024 * c, 1024 * c + 1024), OP.subtract)
+            act(sl, sl, AF.Abs)
+        else:
+            act(sl, src, AF.Copy)
+            for h in range(2):
+                lo = 1024 * c + 512 * h
+                mm(X("pX%d" % h), X("idh"), X("dm", lo, lo + 512), True, False)
+                mm(X("pX%d" % h), X("idn"), X(rep, lo, lo + 512), False, True)
+            for h in range(2):
+                lo = 1024 * c + 512 * h
+                act(X("dm", lo, lo + 512), X("pX%d" % h), AF.Abs)
+        if c % 2:
+            late.append(c // 2)
+
+    def flush():
+        while late:
+            j = late.pop(0)
+            blk = X("pK", 128 * j, 128 * j + 128)
+            mm(blk, X("cdf", 128 * j, 128 * j + 128), X("id1"), True, False)
+            mm(blk, X("eq", 128 * j, 128 * j + 128), X("idb"), False, False)
+            for k in range(16):
+                mm(X("pK", 128 * j + k, 128 * j + 128, 16), X("dm", 2048 * j + k, 2048 * j + 2048, 16), X("g8"), False, k == 15)
+
+    done = {0: 0, 1: 0, 2: 0, 3: 8}
+
+    def fill(t, n):
+        for _ in range(n):
+            flush()
+            if done[t] < 8:
+                chunk(t, done[t])
+                done[t] += 1
+
+    def lists(c, offs, who, base, n):
+        src = ind(X("morw", MO, 4624) if base else X("morw", MO, MD), X(offs, n * c // 16, n * c // 16 + n // 16))
+        out = X("gd", n * c, n * c + n)
+        if who == "s":
+            act(out, src, AF.Copy)
+        else:
+            cp(out, src)
+
+    flip = [0]
+
+    def wide(c, dist, mv, n=1024):
+        lo = (c % (2048 // n)) * n
+        w = n // 16
+        scan(X("es", lo, lo + n), X("rm", 0, n), X("gd", n * c, n * c + n), 0.0, OP.mult, OP.max)
+        flip[0] ^= 1
+        px = X("pX%d" % flip[0], 0, w)
+        mm(px, X("idh"), X("es", lo + 15, lo + n, 16), True, False)
+        mm(px, X("idn"), X(mv, w * c, w * c + w), False, True)
+        act(X(dist, w * c, w * c + w), px, AF.Abs)
+
+    def tl_a(par):
+        tt(X("neq"), X("dri%d" % par, 0, 512), X("basi", par, 1024, 2), OP.not_equal)
+        mm(X("pC"), X("tri"), X("neq"), True, True)
+        act(X("sg"), X("pC"), AF.Sign, bias=X("thr"))
+        act(X("pC"), X("sg"), AF.Copy, bias=2048.0, scale=2048.0)
+
+    def tl_b(par):
+        tt(X("tl", par, 1024, 2), X("pC"), X("dri%d" % par, 0, 512), OP.add)
+
+    def z_tab(par):
+        mm(X("pM"), X("wz"), X("mvt%d" % par, 0, 512), True, True)
+        cp(X("kin", 0, 512), X("pM"))
+        ts(X("kin", 0, 512), X("kin", 0, 512), 3, OP.bitwise_and)
+        cp(X("junk"), X("kin", 0, 512))
+        for b in range(16):
+            mm(X("pU", 256, 288), X("dg", 128 * b, 128 * b + 128), X("junk", b, 512, 16), b == 0, b == 15)
+        cp(X("zw%d" % par), X("pU", 256, 288))
+
+    cp(X("mvt0", 0, 512), X("meas", 0, 1024, 2))
+    for c in range(4):
+        cp(X("zsp", 0, 2048, 16), X("mvt0", 128 * c, 128 * c + 128))
+        scan(X("rep0", 2048 * c, 2048 * c + 2048), X("rm"), X("zsp"), 0.0, OP.mult, OP.add)
+    kap(0)
+    prep(0)
+    fill(0, 1)
+    cp(X("dri0", 0, 512), X("deri", 0, 1024, 2))
+    cp(X("dro0"), X("dri0", 0, 512))
+    fill(0, 1)
+    ms(X("bm"), -1.0)
+    ms(X("tri"), 1.0)
+    ms(X("dg"), 1.0)
+    ms(X("dri0", 512, 640), 0)
+    ms(X("dri1", 512, 640), 0)
+    ms(X("mvt1", 512, 640), 0.0)
+    cp(X("mvt1", 0, 512), X("meas", 1, 1024, 2))
+    same(X("bm"), [], [[0, 16]])
+    same(X("tri"), [], [[0, 16]])
+    asel(X("tri"), [[1, 128]], OP.is_ge, 0, -1)
+
+    def setup_a():
+        cp(X("usef"), X("usei"))
+        send(X("usef"), "uq0", 0, 1)
+        ts(X("pk"), X("pi"), 15, OP.bitwise_and)
+        ts(X("thr"), X("pk", 0, 1), 15, OP.is_ge, 1.5, OP.mult)
+        ts(X("thr"), X("thr"), -0.5, OP.add)
+        tl_a(0)
+        cp(X("dri1", 0, 512), X("deri", 1, 1024, 2))
+        ms(X("tl", 1024, 2048), 6144.0)
+        ms(X("m8r"), 1.0)
+        ms(X("m8r", 0, 256, 8), 0.0)
+        tl_b(0)
+        tl_a(1)
+        for par in range(2):
+            ts(X("bst%d" % par, 0, 512), X("basi", par, 1024, 2), 2048.0, OP.add)
+            ms(X("bst%d" % par, 512, 640), 2048.0)
+        ms(X("morw", MX, 4624), 16384.0)
+        ms(X("marg"), 0.0)
+        ms(X("on"), 1.0)
+        tl_b(1)
+        tt(X("iw"), X("pk"), X("i16"), OP.add)
+        ts(X("bj"), X("iw", 0, 8), 0.5, OP.add)
+        ts(X("j2"), X("iw", 0, 8), 2.0, OP.mult)
+        send(X("tl", 0, 1024), "tq0", 0, 2)
+        iota(X("xr"), [[2, 1024], [-1, 2]], 1, 0, True)
+        iota(X("vr1"), [[2, 512]], 1, 0, True)
+        asel(X("dg"), [[0, 16], [-16, 8], [-1, 16]], OP.is_equal, 0, 1)
+        asel(X("dg"), [[-1, 16], [0, 8], [1, 16]], OP.is_equal, 0, 0)
+        send(X("meas"), "mq1", 1, 3)
+        send(X("meas"), "mq2", 2, 6)
+        for k in range(16):
+            emit("g", lambda e: e.affine_select(T.rep1[:, k:8192:16], T.mvt1[:, 0:512], [[0, 512]], OP.is_ge, 0.0, 1, 0), [X("mvt1", 0, 512)],
+                 [X("rep1", k, 8177 + k)] if k else [X("rep1")])
+
+    def setup_b():
+        ms(X("gds", 512, 640), -100000.0)
+        ms(X("got", 512, 640), 0.0)
+        ms(X("cq", 512, 640), 0.0)
+        ts(X("kin"), X("kin"), 15, OP.bitwise_and)
+        ts(X("km"), X("kin"), 0, OP.is_equal)
+        kap(1)
+        kap(2)
+
+    def setup_c():
+        cp(X("dro1"), X("dri1", 0, 512))
+        ts(X("jp"), X("pk", 0, 1), 1.0, OP.add)
+        ts(X("wz"), X("b1"), X("jp"), OP.mult)
+        z_tab(0)
+        z_tab(1)
+
+    for t in range(3):
+        par = t % 2
+        mvt, bst, dri = "mvt%d" % par, "bst%d" % par, "dri%d" % par
+        for c in range(4):
+            lists(c, "dro%d" % par, DSPLIT[t][c], 0, 2048)
+            if t and c == 0:
+                tl_a(1 - par)
+            fill(t, 2 if c < 3 else 8)
+            if t == 0 and c == 2:
+                setup_a()
+            if t and c == 1:
+                tl_b(1 - par)
+                send(X("tl", 0, 1024), "tq%d" % t, t, 5 if t == 1 else 8)
+            if 1 <= c < 3:
+                wide(c - 1, "dd", mvt, 2048)
+        flush()
+        scan(X("ks"), X("minm"), X("pK"), BIG, OP.max, OP.min)
+        for a in range(8):
+            mm(X("pU", 32 * a, 32 * a + 32), X("la", 128 * a, 128 * a + 128), X("ks", 15, 512, 16), True, True)
+        wide(2, "dd", mvt, 2048)
+        tt(X("um"), X("pU", 0, 256), X("m8"), OP.mult)
+        wide(3, "dd", mvt, 2048)
+        mm(X("pD"), X("b1"), X("dd"), True, True)
+        mm(X("pG"), X("bm"), X("dd"), True, False)
+        scan(X("us"), X("m8r"), X("um"), 0.0, OP.mult, OP.add)
+        for h in range(2):
+            for j in (2 * h, 2 * h + 1):
+                cp(X("wi", 8 * j, 8 * j + 8), X("us", 8 * j + 7, 256, 32))
+            w = (16 * h, 16 * h + 16)
+            ts(X("wj", *w), X("wi", *w), 2047, OP.bitwise_and)
+            cp(X("wo", *w), X("wj", *w))
+            l = (256 * h, 256 * h + 256)
+            tt(X("ec", *l), ind(X("tl"), X("wo", *w)), X(bst, *l), OP.max)
+            ts(X("eo", *l), X("ec", *l), -2048.0, OP.add)
+            for c in range(4):
+                if ESPLIT[c] == "s" and not h:
+                    lists(c, "eo", "s", 1, 1024)
+        if t == 0:
+            setup_b()
+        us = X("usef", 37 * t, 37 * t + 512)
+        for c in range(8):
+            if ESPLIT[c] == "v":
+                lists(c, "eo", "v", 1, 1024)
+            if c < 4 and ESPLIT[c + 4] == "s":
+                lists(c + 4, "eo", "s", 1, 1024)
+            wide(c, "ee", mvt)
+            if c == 2:
+                cp(X("dk"), ind(X("xr"), X("wo")))
+            if c == 4:
+                tt(X("pM"), X("dk"), us, OP.subtract)
+                tt(X("dk"), X("pM"), X("km", t, t + 512), OP.mult)
+        mm(X("pG"), X("b1"), X("ee"), False, True)
+        ts(X("fail"), X("pG"), X("marg"), OP.add, 0.0, OP.is_ge)
+        scan(X("cum"), X("fail"), X("fail"), 0.0, OP.add, OP.max)
+        for a in range(8):
+            act(X("junk"), X("cum"), AF.Sign, bias=X("bj", a, a + 1), scale=-1.0, accum=X("acc", a, a + 1))
+        act(X("cq", 0, 512), ind(X("uq%d" % t), X("kap%d" % t)), AF.Copy)
+        act(X("gds", 0, 512), X("pD"), AF.Copy)
+        act(X("got", 0, 512), X("fail"), AF.Copy, bias=1.0, scale=-1.0)
+        ts(X("pC"), X("fail"), -1.0, OP.mult, 1.0, OP.add)
+        tt(X("pM"), X("dk"), X("pC"), OP.mult)
+        tt(us, X("pM"), us, OP.add)
+        if t < 2:
+            send(X("usef"), "uq%d" % (t + 1), t + 1, 4 if t == 0 else 7)
+            prep(t + 1)
+        else:
+            dma("y", T.yu[:], T.usef[:], R=[X("usef")])
+        tt(X("pM"), X("ec"), X("pC"), OP.mult)
+        tt(X("nd", 0, 512), X("pM"), X(dri, 0, 512), OP.max)
+        ms(X("nd", 512, 640), 0)
+        if t == 0:
+            setup_c()
+        fill(t + 1, FILL[0] - (2 if t == 0 else 0))
+        ts(X("sm"), X("acc"), 511.0, OP.is_gt)
+        tt(X("sm"), X("sm"), X("j2"), OP.mult)
+        tt(X("sm"), X("sm"), X("acc"), OP.add)
+        ts(X("sel"), X("sm"), 0.5, OP.mult, 256.0, OP.add)
+        cp(X("c2f"), ind(X("cq"), X("sel")))
+        cp(X("c2o"), X("c2f"))
+        cp(X("mv2"), ind(X(mvt), X("sel")))
+        cp(X("zsp", 0, 2048, 16), X("mv2"))
+        scan(X("rp2"), X("rm"), X("zsp"), 0.0, OP.mult, OP.add)
+        mm(X("pC", 0, 128), X("c2f"), X("id1"), True, False)
+        for h in range(2):
+            l = (1024 * h, 1024 * h + 1024)
+            d2 = X("gd", 4096 + 1024 * h, 5120 + 1024 * h)
+            tt(d2, ind(X("mq%d" % t), X("c2o", 64 * h, 64 * h + 64)), X("rp2", *l), OP.subtract)
+            act(d2, d2, AF.Abs)
+        for k in range(16):
+            mm(X("pC", k, 128, 16), X("gd", 4096 + k, 6144, 16), X("g8"), False, k == 15)
+        act(X("gd2"), ind(X("gds"), X("sel")), AF.Copy)
+        cp(X("bs2"), ind(X(bst), X("sel")))
+        cp(X("dr2"), ind(X(dri), X("sel")))
+        fill(t + 1, FILL[1])
+        scan(X("ks2"), X("minm", 0, 128), X("pC", 0, 128), BIG, OP.max, OP.min)
+        for a in range(8):
+            mm(X("pU", 8 * a, 8 * a + 8), X("la", 128 * a, 128 * a + 128), X("ks2", 15, 128, 16), True, True)
+        fill(t + 1, FILL[2])
+        tt(X("um2"), X("pU", 0, 64), X("m8", 0, 64), OP.mult)
+        scan(X("us2"), X("m8r", 0, 64), X("um2"), 0.0, OP.mult, OP.add)
+        cp(X("wi", 0, 8), X("us2", 7, 64, 8))
+        ts(X("wj", 0, 8), X("wi", 0, 8), 2047, OP.bitwise_and)
+        cp(X("w2o"), X("wj", 0, 8))
+        tt(X("ec2"), ind(X("tq%d" % t), X("w2o")), X("bs2"), OP.max)
+        ts(X("eo2"), X("ec2"), -2048.0, OP.add)
+        lists(0, "eo2", "s", 1, 1024)
+        lists(1, "eo2", "v", 1, 1024)
+        wide(0, "ee2", "mv2")
+        wide(1, "ee2", "mv2")
+        mm(X("pD", 0, 128), X("b1"), X("ee2"), True, True)
+        cp(X("zi"), X("zw%d" % par))
+        ts(X("zt"), X("zi"), t, OP.add)
+        ts(X("zu"), X("zt"), 3, OP.bitwise_and)
+        ts(X("zc"), X("iw"), 3.0, OP.mult, float(MO), OP.add)
+        tt(X("zc"), X("zc"), X("zu"), OP.add)
+        fill(t + 1, FILL[3])
+        tt(X("x2"), X("pD", 0, 128), X("gd2"), OP.subtract)
+        ts(X("ad2"), X("x2"), X("marg"), OP.add, 0.0, OP.is_lt)
+        cp(ind(X("got"), X("sel")), X("ad2"))
+        for b in range(16):
+            mm(X("pU", 256, 288), X("dg", 128 * b, 128 * b + 128), X("got", b, 512, 16), b == 0, b == 15)
+        tt(X("y2"), X("ad2"), X("ec2"), OP.mult)
+        tt(X("n2"), X("y2"), X("dr2"), OP.max)
+        tt(X("gf"), X("pU", 256, 288), X("zc"), OP.mult)
+        tt(X("gf"), X("gf"), X("iw"), OP.add)
+        cp(X("gu"), X("gf"))
+        cp(ind(X("morw", 0, MD), X("gu")), X(mvt, 0, 512))
+        if t < 2:
+            emit("v", lambda e: e.tensor_reduce(T.cn[:], T.pU[:, 256:288], AxisListType.X, OP.add), [X("pU", 256, 288)], [X("cn")])
+            mm(X("pC", 0, 1), X("on"), X("cn"), True, True)
+            dma("y", T.morw[:, MD:MX], T.morw[:, MO:MD], R=[X("morw", MO, MD)], W=[X("morw", MD, MX)])
+        else:
+            dma("s", T.ym[:], T.morw[:, MO:MD], R=[X("morw", MO, MD)])
+        cp(ind(X("nd"), X("sel")), X("n2"))
+        ts(X(dri), X("nd"), 2047, OP.bitwise_and)
+        if t < 2:
+            cp(X("wi", 0, 1), X("pC", 0, 1))
+            ts(X("wj", 0, 1), X("wi", 0, 1), 127, OP.bitwise_and)
+            cp(X("marg"), X("wj", 0, 1))
+            if t == 0:
+                cp(X("dro0"), X("dri0", 0, 512))
+        if t > 0:
+            cp(X("ydb", par, 1024, 2), X(dri, 0, 512))
+    dma("y", T.yd[:], T.ydb[:], R=[X("ydb")])
+    for s in sorted(total):
+        if clock["g"].get(s, 0) < total[s]:
+            g.wait_ge(T.sem[s], total[s])

@@ -30,7 +30,7 @@ _buf("gf zw0 zw1 zc i16 iw", 32, F)
 _buf("cdf eq ks ec dk vr0 vr1 minm", 512, F)
 _buf("um us m8 m8r", 256, F)
 _buf("es rp2 rm zsp dg", 2048, B)
-_buf("dd ee fail cum junk sg neq", 512, B)
+_buf("one dd ee fail cum junk sg neq", 512, B)
 _buf("marg cn thr jp", 1, F)
 _buf("acc sm bj j2", 8, F)
 _buf("sel w2o", 8, U)
@@ -45,10 +45,12 @@ _buf("km", 528, B)
 _buf("pK pU pG pD pC pM pX0 pX1", 512, F, P_)
 SEMAPHORES = ["cv", "cs", "cp", "cg"] + ["d%d" % i for i in range(24)] + ["rl%d" % i for i in range(9)] + ["ar%d" % i for i in range(9)]
 BIG = float(2 ** 25)
-ESPLIT = "ssvsssvs"
-DSPLIT = ("ssss", "svss", "svss")
-MSPLIT = ("vvvvvvvv", "ppvvpvvv", "ppvvpvvv")
-FILL = (4, 1, 1, 2)
+EORD = ("G2 W0 W1 W2 W3 W4 G6 W5 W6 W7", "G3 W0 W1 W2 W3 G7 W4 W5 W6 W7", "G3 W0 W1 W2 W3 G7 W4 W5 W6 W7")
+DSPLIT = ("ssss", "sssv", "sssv")
+MSPLIT = ("pvvvvvvv", "vvvvpvvv", "vpvvvvvv")
+FILL = ((2, 1, 1, 2), (5, 2, 1, 2), (0, 0, 0, 0))
+DFILL = ((2, 2, 2), (0, 2, 1), (2, 2, 2))
+CNTV = (0, 0, 2)
 
 
 def rank_program(g, core, T, topo):
@@ -137,6 +139,9 @@ def rank_program(g, core, T, topo):
     def ms(out, val):
         emit("v", lambda e: e.memset(out[0], val), [], [out])
 
+    def red(out, a):
+        emit("v", lambda e: e.tensor_reduce(out[0], a[0], AxisListType.X, OP.add), [a], [out])
+
     def scan(out, d0, d1, init, op0, op1):
         emit("v", lambda e: e.tensor_tensor_scan(out[0], d0[0], d1[0], init, op0, op1), [d0, d1], [out])
 
@@ -169,10 +174,10 @@ def rank_program(g, core, T, topo):
         log.setdefault(dst, []).append((0, 1024, True, "x", "ar%d" % ix, len(e), {"ar%d" % ix: len(e)}, False, 0))
         total["ar%d" % ix] = len(e)
 
+    dma("y", T.meas[:], T.mea[:], W=[X("meas")], sem="d1")
     for b in range(16):
         dma("y" if b % 2 == 0 else "s", T.b15[b::16, 0:994], T.bas[15::16, 2 * b:2 * b + 994], W=[X("b15")] if b == 15 else [], sem="d0", tot=256)
-    nsem[0] = 1
-    dma("y", T.meas[:], T.mea[:], W=[X("meas")])
+    nsem[0] = 2
     dma("s", T.usei[:], T.use[:], W=[X("usei")])
     dma("y", T.deri[:], T.der[:], W=[X("deri")])
     dma("s", T.morw[:, MO:MD], T.mor[:], W=[X("morw", MO, MD)])
@@ -221,6 +226,14 @@ def rank_program(g, core, T, topo):
 
     late = []
 
+    def sub_abs(name, lo, rep, rlo):
+        for h in range(2):
+            a = X(name, lo + 512 * h, lo + 512 * h + 512)
+            mm(X("pX%d" % h), X("idh"), a, True, False)
+            mm(X("pX%d" % h), X("idn"), X(rep, rlo + 512 * h, rlo + 512 * h + 512), False, True)
+        for h in range(2):
+            act(X(name, lo + 512 * h, lo + 512 * h + 512), X("pX%d" % h), AF.Abs)
+
     def chunk(t, c):
         sl = X("dm", 1024 * c, 1024 * c + 1024)
         rep = "rep%d" % (t % 2)
@@ -230,13 +243,7 @@ def rank_program(g, core, T, topo):
             act(sl, sl, AF.Abs)
         else:
             act(sl, src, AF.Copy)
-            for h in range(2):
-                lo = 1024 * c + 512 * h
-                mm(X("pX%d" % h), X("idh"), X("dm", lo, lo + 512), True, False)
-                mm(X("pX%d" % h), X("idn"), X(rep, lo, lo + 512), False, True)
-            for h in range(2):
-                lo = 1024 * c + 512 * h
-                act(X("dm", lo, lo + 512), X("pX%d" % h), AF.Abs)
+            sub_abs("dm", 1024 * c, rep, 1024 * c)
         if c % 2:
             late.append(c // 2)
 
@@ -297,7 +304,9 @@ def rank_program(g, core, T, topo):
         cp(X("zw%d" % par), X("pU", 256, 288))
 
     cp(X("mvt0", 0, 512), X("meas", 0, 1024, 2))
-    for c in range(4):
+    for k in range(16):
+        act(X("rep0", 4096 + k, 8192, 16), X("mvt0", 256, 512), AF.Copy)
+    for c in range(2):
         cp(X("zsp", 0, 2048, 16), X("mvt0", 128 * c, 128 * c + 128))
         scan(X("rep0", 2048 * c, 2048 * c + 2048), X("rm"), X("zsp"), 0.0, OP.mult, OP.add)
     kap(0)
@@ -307,29 +316,37 @@ def rank_program(g, core, T, topo):
     cp(X("dro0"), X("dri0", 0, 512))
     fill(0, 1)
     ms(X("bm"), -1.0)
+    ms(X("one"), 1.0)
     ms(X("tri"), 1.0)
-    ms(X("dg"), 1.0)
     ms(X("dri0", 512, 640), 0)
     ms(X("dri1", 512, 640), 0)
+    ms(X("nd", 512, 640), 0)
     ms(X("mvt1", 512, 640), 0.0)
     cp(X("mvt1", 0, 512), X("meas", 1, 1024, 2))
     same(X("bm"), [], [[0, 16]])
+    iota(X("tl", 1024, 2048), [[0, 1024]], 6144, 0, True)
     same(X("tri"), [], [[0, 16]])
     asel(X("tri"), [[1, 128]], OP.is_ge, 0, -1)
+    for k in range(16):
+        emit("g", lambda e: e.affine_select(T.rep1[:, k:8192:16], T.mvt1[:, 0:512], [[0, 512]], OP.is_ge, 0.0, 1, 0), [X("mvt1", 0, 512)],
+             [X("rep1")] if k == 15 else [])
 
-    def setup_a():
-        cp(X("usef"), X("usei"))
-        send(X("usef"), "uq0", 0, 1)
+    def setup_0():
         ts(X("pk"), X("pi"), 15, OP.bitwise_and)
         ts(X("thr"), X("pk", 0, 1), 15, OP.is_ge, 1.5, OP.mult)
         ts(X("thr"), X("thr"), -0.5, OP.add)
         tl_a(0)
         cp(X("dri1", 0, 512), X("deri", 1, 1024, 2))
-        ms(X("tl", 1024, 2048), 6144.0)
         ms(X("m8r"), 1.0)
         ms(X("m8r", 0, 256, 8), 0.0)
+
+    def setup_1():
+        cp(X("usef"), X("usei"))
+        send(X("usef"), "uq0", 0, 1)
         tl_b(0)
         tl_a(1)
+
+    def setup_a():
         for par in range(2):
             ts(X("bst%d" % par, 0, 512), X("basi", par, 1024, 2), 2048.0, OP.add)
             ms(X("bst%d" % par, 512, 640), 2048.0)
@@ -343,13 +360,11 @@ def rank_program(g, core, T, topo):
         send(X("tl", 0, 1024), "tq0", 0, 2)
         iota(X("xr"), [[2, 1024], [-1, 2]], 1, 0, True)
         iota(X("vr1"), [[2, 512]], 1, 0, True)
+        iota(X("dg"), [[0, 2048]], 1, 0, True)
         asel(X("dg"), [[0, 16], [-16, 8], [-1, 16]], OP.is_equal, 0, 1)
         asel(X("dg"), [[-1, 16], [0, 8], [1, 16]], OP.is_equal, 0, 0)
         send(X("meas"), "mq1", 1, 3)
         send(X("meas"), "mq2", 2, 6)
-        for k in range(16):
-            emit("g", lambda e: e.affine_select(T.rep1[:, k:8192:16], T.mvt1[:, 0:512], [[0, 512]], OP.is_ge, 0.0, 1, 0), [X("mvt1", 0, 512)],
-                 [X("rep1", k, 8177 + k)] if k else [X("rep1")])
 
     def setup_b():
         ms(X("gds", 512, 640), -100000.0)
@@ -374,9 +389,9 @@ def rank_program(g, core, T, topo):
             lists(c, "dro%d" % par, DSPLIT[t][c], 0, 2048)
             if t and c == 0:
                 tl_a(1 - par)
-            fill(t, 2 if c < 3 else 8)
-            if t == 0 and c == 2:
-                setup_a()
+            fill(t, DFILL[t][c] if c < 3 else 8)
+            if t == 0 and c < 3:
+                (setup_0, setup_1, setup_a)[c]()
             if t and c == 1:
                 tl_b(1 - par)
                 send(X("tl", 0, 1024), "tq%d" % t, t, 5 if t == 1 else 8)
@@ -392,6 +407,14 @@ def rank_program(g, core, T, topo):
         mm(X("pD"), X("b1"), X("dd"), True, True)
         mm(X("pG"), X("bm"), X("dd"), True, False)
         scan(X("us"), X("m8r"), X("um"), 0.0, OP.mult, OP.add)
+        mine = [c for c in range(8) if "G%d" % c not in EORD[t]]
+        ahead = []
+
+        def gather_e(n, top):
+            for c in [c for c in mine if c not in ahead and c < top][:n]:
+                lists(c, "eo", "s", 1, 1024)
+                ahead.append(c)
+
         for h in range(2):
             for j in (2 * h, 2 * h + 1):
                 cp(X("wi", 8 * j, 8 * j + 8), X("us", 8 * j + 7, 256, 32))
@@ -401,17 +424,18 @@ def rank_program(g, core, T, topo):
             l = (256 * h, 256 * h + 256)
             tt(X("ec", *l), ind(X("tl"), X("wo", *w)), X(bst, *l), OP.max)
             ts(X("eo", *l), X("ec", *l), -2048.0, OP.add)
-            for c in range(4):
-                if ESPLIT[c] == "s" and not h:
-                    lists(c, "eo", "s", 1, 1024)
+            if h == 0:
+                gather_e(4, 4)
         if t == 0:
             setup_b()
         us = X("usef", 37 * t, 37 * t + 512)
-        for c in range(8):
-            if ESPLIT[c] == "v":
+        gather_e(4 - len(ahead), 8)
+        for tok in EORD[t].split():
+            c = int(tok[1])
+            if tok[0] == "G":
                 lists(c, "eo", "v", 1, 1024)
-            if c < 4 and ESPLIT[c + 4] == "s":
-                lists(c + 4, "eo", "s", 1, 1024)
+                continue
+            gather_e(1, 8)
             wide(c, "ee", mvt)
             if c == 2:
                 cp(X("dk"), ind(X("xr"), X("wo")))
@@ -421,12 +445,13 @@ def rank_program(g, core, T, topo):
         mm(X("pG"), X("b1"), X("ee"), False, True)
         ts(X("fail"), X("pG"), X("marg"), OP.add, 0.0, OP.is_ge)
         scan(X("cum"), X("fail"), X("fail"), 0.0, OP.add, OP.max)
-        for a in range(8):
+        for a in range(8 - CNTV[t]):
             act(X("junk"), X("cum"), AF.Sign, bias=X("bj", a, a + 1), scale=-1.0, accum=X("acc", a, a + 1))
         act(X("cq", 0, 512), ind(X("uq%d" % t), X("kap%d" % t)), AF.Copy)
         act(X("gds", 0, 512), X("pD"), AF.Copy)
         act(X("got", 0, 512), X("fail"), AF.Copy, bias=1.0, scale=-1.0)
-        ts(X("pC"), X("fail"), -1.0, OP.mult, 1.0, OP.add)
+        mm(X("pC"), X("idn"), X("fail"), True, False)
+        mm(X("pC"), X("idh"), X("one"), False, True)
         tt(X("pM"), X("dk"), X("pC"), OP.mult)
         tt(us, X("pM"), us, OP.add)
         if t < 2:
@@ -436,10 +461,13 @@ def rank_program(g, core, T, topo):
             dma("y", T.yu[:], T.usef[:], R=[X("usef")])
         tt(X("pM"), X("ec"), X("pC"), OP.mult)
         tt(X("nd", 0, 512), X("pM"), X(dri, 0, 512), OP.max)
-        ms(X("nd", 512, 640), 0)
+        for a in range(8 - CNTV[t], 8):
+            ts(X("neq"), X("cum"), X("bj", a, a + 1), OP.is_le)
+            red(X("acc", a, a + 1), X("neq"))
+            ts(X("acc", a, a + 1), X("acc", a, a + 1), 2.0, OP.mult, -512.0, OP.add)
         if t == 0:
             setup_c()
-        fill(t + 1, FILL[0] - (2 if t == 0 else 0))
+        fill(t + 1, FILL[t][0])
         ts(X("sm"), X("acc"), 511.0, OP.is_gt)
         tt(X("sm"), X("sm"), X("j2"), OP.mult)
         tt(X("sm"), X("sm"), X("acc"), OP.add)
@@ -450,21 +478,20 @@ def rank_program(g, core, T, topo):
         cp(X("zsp", 0, 2048, 16), X("mv2"))
         scan(X("rp2"), X("rm"), X("zsp"), 0.0, OP.mult, OP.add)
         mm(X("pC", 0, 128), X("c2f"), X("id1"), True, False)
-        for h in range(2):
-            l = (1024 * h, 1024 * h + 1024)
-            d2 = X("gd", 4096 + 1024 * h, 5120 + 1024 * h)
-            tt(d2, ind(X("mq%d" % t), X("c2o", 64 * h, 64 * h + 64)), X("rp2", *l), OP.subtract)
-            act(d2, d2, AF.Abs)
+        act(X("gd", 5120, 6144), ind(X("mq%d" % t), X("c2o", 64, 128)), AF.Copy)
+        tt(X("gd", 4096, 5120), ind(X("mq%d" % t), X("c2o", 0, 64)), X("rp2", 0, 1024), OP.subtract)
+        sub_abs("gd", 5120, "rp2", 1024)
+        act(X("gd", 4096, 5120), X("gd", 4096, 5120), AF.Abs)
         for k in range(16):
             mm(X("pC", k, 128, 16), X("gd", 4096 + k, 6144, 16), X("g8"), False, k == 15)
         act(X("gd2"), ind(X("gds"), X("sel")), AF.Copy)
         cp(X("bs2"), ind(X(bst), X("sel")))
         cp(X("dr2"), ind(X(dri), X("sel")))
-        fill(t + 1, FILL[1])
+        fill(t + 1, FILL[t][1])
         scan(X("ks2"), X("minm", 0, 128), X("pC", 0, 128), BIG, OP.max, OP.min)
         for a in range(8):
             mm(X("pU", 8 * a, 8 * a + 8), X("la", 128 * a, 128 * a + 128), X("ks2", 15, 128, 16), True, True)
-        fill(t + 1, FILL[2])
+        fill(t + 1, FILL[t][2])
         tt(X("um2"), X("pU", 0, 64), X("m8", 0, 64), OP.mult)
         scan(X("us2"), X("m8r", 0, 64), X("um2"), 0.0, OP.mult, OP.add)
         cp(X("wi", 0, 8), X("us2", 7, 64, 8))
@@ -482,7 +509,7 @@ def rank_program(g, core, T, topo):
         ts(X("zu"), X("zt"), 3, OP.bitwise_and)
         ts(X("zc"), X("iw"), 3.0, OP.mult, float(MO), OP.add)
         tt(X("zc"), X("zc"), X("zu"), OP.add)
-        fill(t + 1, FILL[3])
+        fill(t + 1, FILL[t][3])
         tt(X("x2"), X("pD", 0, 128), X("gd2"), OP.subtract)
         ts(X("ad2"), X("x2"), X("marg"), OP.add, 0.0, OP.is_lt)
         cp(ind(X("got"), X("sel")), X("ad2"))
@@ -495,7 +522,7 @@ def rank_program(g, core, T, topo):
         cp(X("gu"), X("gf"))
         cp(ind(X("morw", 0, MD), X("gu")), X(mvt, 0, 512))
         if t < 2:
-            emit("v", lambda e: e.tensor_reduce(T.cn[:], T.pU[:, 256:288], AxisListType.X, OP.add), [X("pU", 256, 288)], [X("cn")])
+            red(X("cn"), X("pU", 256, 288))
             mm(X("pC", 0, 1), X("on"), X("cn"), True, True)
             dma("y", T.morw[:, MD:MX], T.morw[:, MO:MD], R=[X("morw", MO, MD)], W=[X("morw", MD, MX)])
         else:

from concourse.mybir import AluOpType as OP, AxisListType, ActivationFunctionType as AF

S_, P_ = "sbuf", "psum"
F, B, I, U = "float32", "bfloat16", "int32", "uint16"
MO, MD, MX = 512, 2560, 4608
SCRATCH = {}


def _buf(names, n, d, where=S_):
    for x in names.split():
        SCRATCH[x] = (where, [128, n], d)


_buf("b15", 994, I)
_buf("basi deri usei", 1024, I)
_buf("meas", 1024, B)
_buf("morw", 4624, B)
_buf("usef ydb", 1024, F)
_buf("tl xr", 2048, F)
_buf("mvt0 mvt1 got", 640, B)
_buf("bst0 bst1 gds cq", 640, F)
_buf("dri0 dri1 nd", 640, I)
_buf("dro0 dro1 cdo eo", 512, U)
_buf("rep0 rep1 dm gd", 8192, B)
_buf("mq0 mq1 mq2", 1024, B)
_buf("uq0 uq1 uq2 tq0 tq1 tq2", 1024, F)
_buf("wi wj pi pk zi zt zu", 32, I)
_buf("kap0 kap1 kap2 wo gu", 32, U)
_buf("gf zw0 zw1 zc i16 iw", 32, F)
_buf("cdf eq ks ec dk vr0 vr1 minm", 512, F)
_buf("um us m8 m8r", 256, F)
_buf("es rp2 rm zsp dg", 2048, B)
_buf("one dd ee fail cum junk sg neq", 512, B)
_buf("marg cn thr jp", 1, F)
_buf("acc sm bj j2", 8, F)
_buf("sel w2o", 8, U)
_buf("c2f bs2 gd2 dr2 ks2 ec2 x2 ad2 y2 n2 id1 idb on", 128, F)
_buf("c2o eo2", 128, U)
_buf("mv2 ee2 b1 bm tri idh idn wz", 128, B)
_buf("um2 us2", 64, F)
_buf("g8", 8, B)
_buf("la", 1024, F)
_buf("kin", 528, I)
_buf("km", 528, B)
_buf("pK pU pG pD pC pM pX0 pX1", 512, F, P_)
SEMAPHORES = ["cv", "cs", "cp", "cg"] + ["d%d" % i for i in range(24)] + ["rl%d" % i for i in range(9)] + ["ar%d" % i for i in range(9)]
BIG = float(2 ** 25)
EORD = ("G2 W0 W1 W2 W3 W4 G6 W5 W6 W7", "G3 W0 W1 W2 W3 G7 W4 W5 W6 W7", "G3 W0 W1 W2 W3 G7 W4 W5 W6 W7")
DSPLIT = ("ssss", "sssv", "sssv")
MSPLIT = ("pvvvvvvv", "vvvvpvvv", "vpvvvvvv")
FILL = ((2, 1, 1, 2), (5, 2, 1, 2), (0, 0, 0, 0))
DFILL = ((2, 2, 2), (0, 2, 1), (2, 2, 2))
CNTV = (0, 0, 2)


def rank_program(g, core, T, topo):
    rank = T.rank_of(core)
    if rank is None:
        return
    queue = {"v": g.vector, "s": g.scalar, "p": g.tensor, "g": g, "y": g.sync}
    clock = {q: {} for q in queue}
    total, log, nd = {}, {}, [0]

    def X(name, lo=0, hi=None, st=None):
        hi = SCRATCH[name][1][1] if hi is None else hi
        return (T[name][:, lo:hi] if st is None else T[name][:, lo:hi:st], name, lo, hi)

    def emit(q, fn, R, W, sem=None, n=1, tot=None):
        deps = []
        touch = [(v[1], v[2], v[3], False) for v in R] + [(v[1], v[2], v[3], True) for v in W]
        for name, lo, hi, w in touch:
            ps = SCRATCH[name][0] == "psum"
            for rec in log.get(name, []):
                if not ps and (rec[1] <= lo or hi <= rec[0]):
                    continue
                if not (w or rec[2] or ps):
                    continue
                if rec[3] == q and sem is None and rec[7]:
                    if q == "p" or not (w or rec[2]) or rec[1] <= lo or hi <= rec[0]:
                        continue
                deps.append(rec)
        for rec in sorted(deps, key=lambda r: -r[8]):
            if clock[q].get(rec[4], 0) < rec[5]:
                queue[q].wait_ge(T.sem[rec[4]], rec[5])
                for s, c in rec[6].items():
                    clock[q][s] = max(clock[q].get(s, 0), c)
        comp = sem is None
        s = {"v": "cv", "s": "cs", "p": "cp", "g": "cg"}[q] if comp else sem
        ins = fn(queue[q])
        if n:
            ins.then_inc(T.sem[s], n)
        total[s] = total.get(s, 0) + n if comp else (tot or n)
        c = dict(clock[q])
        c[s] = total[s]
        nd[0] += 1
        for name, lo, hi, w in touch:
            recs = log.setdefault(name, [])
            if w:
                recs = [r for r in recs if not (lo <= r[0] and r[1] <= hi)]
            else:
                recs = [r for r in recs if not (r[3] == q and comp and r[7] and not r[2] and lo <= r[0] and r[1] <= hi)]
            recs.append((lo, hi, w, q, s, total[s], c, comp, nd[0]))
            log[name] = recs

    nsem = [0]

    def dma(q, out, in_, R=(), W=(), sem=None, tot=None):
        if sem is None:
            sem = "d%d" % nsem[0]
            nsem[0] += 1
        emit(q, lambda e: e.dma_start(out, in_), R, W, sem=sem, n=16, tot=tot or 16)

    def ind(win, off):
        return (win[0].indirect(off[0]), win, off)

    def rd(*vs):
        r = []
        for v in vs:
            r += [v[1], v[2]] if len(v) == 3 else [v]
        return r

    def tt(out, a, b, op):
        emit("v", lambda e: e.tensor_tensor(out[0], a[0], b[0], op), rd(a, b), [out])

    def ts(out, a, s1, op0, s2=None, op1=None):
        R = rd(a) + ([s1] if isinstance(s1, tuple) else [])
        k1 = s1[0] if isinstance(s1, tuple) else s1
        if op1 is None:
            emit("v", lambda e: e.tensor_scalar(out[0], a[0], k1, None, op0), R, [out])
        else:
            emit("v", lambda e: e.tensor_scalar(out[0], a[0], k1, s2, op0, op1), R, [out])

    def cp(out, a):
        if len(out) == 3:
            emit("v", lambda e: e.tensor_copy(out[0], a[0]), rd(a) + [out[2]], [out[1]])
        else:
            emit("v", lambda e: e.tensor_copy(out[0], a[0]), rd(a), [out])

    def ms(out, val):
        emit("v", lambda e: e.memset(out[0], val), [], [out])

    def red(out, a):
        emit("v", lambda e: e.tensor_reduce(out[0], a[0], AxisListType.X, OP.add), [a], [out])

    def scan(out, d0, d1, init, op0, op1):
        emit("v", lambda e: e.tensor_tensor_scan(out[0], d0[0], d1[0], init, op0, op1), [d0, d1], [out])

    def act(out, a, func, bias=0.0, scale=1.0, accum=None):
        R = rd(a) + ([bias] if isinstance(bias, tuple) else [])
        k = bias[0] if isinstance(bias, tuple) else bias
        if accum:
            emit("s", lambda e: e.activation(out[0], a[0], func, bias=k, scale=scale, accum_out=accum[0]), R, [out, accum])
        else:
            emit("s", lambda e: e.activation(out[0], a[0], func, bias=k, scale=scale), R, [out])

    def mm(out, l, r, start, stop):
        emit("p", lambda e: e.matmul(out[0], l[0], r[0], start, stop), [l, r], [out])

    def iota(out, pat, base, cm, flt):
        emit("g", lambda e: e.iota(out[0], pat, base, cm, allow_small_or_imprecise_dtypes=True) if flt else e.iota(out[0], pat, base, cm), [], [out])

    def asel(b, pat, op, base, cm):
        emit("g", lambda e: e.affine_select(b[0], b[0], pat, op, 0.0, base, cm), [b], [b])

    cores = T.cores

    def send(src, dst, t, ix):
        to = cores[(rank - 1 - t) % len(cores)]
        e = topo.engines(core, to)[:8]
        m = sum(1 << k for k in e)
        a = topo.addr(to)
        out = T[dst][:, 0:1024]
        emit("g", lambda q: q.remote_dma(out, src[0], T.sem["ar%d" % ix], T.sem["rl%d" % ix], a[1], a[0], m), [src], [], sem="rl%d" % ix, n=0, tot=len(e))
        log.setdefault(dst, []).append((0, 1024, True, "x", "ar%d" % ix, len(e), {"ar%d" % ix: len(e)}, False, 0))
        total["ar%d" % ix] = len(e)

    dma("y", T.meas[:], T.mea[:], W=[X("meas")], sem="d1")
    for b in range(16):
        dma("y" if b % 2 == 0 else "s", T.b15[b::16, 0:994], T.bas[15::16, 2 * b:2 * b + 994], W=[X("b15")] if b == 15 else [], sem="d0", tot=256)
    nsem[0] = 2
    dma("s", T.usei[:], T.use[:], W=[X("usei")])
    dma("y", T.deri[:], T.der[:], W=[X("deri")])
    dma("s", T.morw[:, MO:MD], T.mor[:], W=[X("morw", MO, MD)])
    dma("y", T.basi[:], T.bas[:], W=[X("basi")])
    dma("y", T.morw[:, MD:MX], T.mor[:], W=[X("morw", MD, MX)])

    def same(b, o, st):
        asel(b, o + [[-16, 8]] + st, OP.is_ge, 0, 1)
        asel(b, o + [[16, 8]] + st, OP.is_ge, 15, -1)

    ms(X("rm"), 1.0)
    ms(X("zsp"), 0.0)
    ms(X("rm", 0, 2048, 16), 0.0)
    ms(X("g8"), 2048.0)
    ms(X("id1"), 1.0)
    ms(X("idb"), float(2 ** 23 + 1024))
    ms(X("mvt0", 512, 640), 0.0)
    ms(X("idh"), 1.0)
    ms(X("idn"), -1.0)
    ms(X("minm"), 0.0)
    ms(X("la"), 1.0)
    ms(X("minm", 0, 512, 16), BIG)
    ms(X("m8"), 1.0)
    ms(X("b1"), 1.0)
    same(X("g8"), [], [])
    for n in ("id1", "idb", "idh", "idn"):
        asel(X(n), [[-1, 128]], OP.is_equal, 0, 1)
    iota(X("vr0"), [[2, 512]], 0, 0, True)
    iota(X("pi"), [[0, 32]], 0, 1, False)
    send(X("meas"), "mq0", 0, 0)
    asel(X("la"), [[-16, 8], [0, 8], [-1, 16]], OP.is_equal, 0, 1)
    same(X("m8"), [[0, 32]], [])
    same(X("b1"), [], [[0, 16]])
    iota(X("i16"), [[16, 32]], 0, 0, True)
    iota(X("kin"), [[-1, 528]], 1024, 1, False)

    def kap(t):
        ts(X("zt"), X("b15", t % 2, 994, 32), 97 * t, OP.add)
        ts(X("zu"), X("zt"), 1023, OP.bitwise_and)
        cp(X("kap%d" % t), X("zu"))

    def prep(t):
        cp(X("cdf"), ind(X("usef") if t else X("usei"), X("kap%d" % t)))
        cp(X("cdo"), X("cdf"))
        tt(X("eq"), X("cdf"), X("vr%d" % (t % 2)), OP.is_equal)

    late = []

    def sub_abs(name, lo, rep, rlo):
        for h in range(2):
            a = X(name, lo + 512 * h, lo + 512 * h + 512)
            mm(X("pX%d" % h), X("idh"), a, True, False)
            mm(X("pX%d" % h), X("idn"), X(rep, rlo + 512 * h, rlo + 512 * h + 512), False, True)
        for h in range(2):
            act(X(name, lo + 512 * h, lo + 512 * h + 512), X("pX%d" % h), AF.Abs)

    def chunk(t, c):
        sl = X("dm", 1024 * c, 1024 * c + 1024)
        rep = "rep%d" % (t % 2)
        src = ind(X("meas"), X("cdo", 64 * c, 64 * c + 64))
        if MSPLIT[t][c] == "v":
            tt(sl, src, X(rep, 1024 * c, 1024 * c + 1024), OP.subtract)
            act(sl, sl, AF.Abs)
        else:
            act(sl, src, AF.Copy)
            sub_abs("dm", 1024 * c, rep, 1024 * c)
        if c % 2:
            late.append(c // 2)

    def flush():
        while late:
            j = late.pop(0)
            blk = X("pK", 128 * j, 128 * j + 128)
            mm(blk, X("cdf", 128 * j, 128 * j + 128), X("id1"), True, False)
            mm(blk, X("eq", 128 * j, 128 * j + 128), X("idb"), False, False)
            for k in range(16):
                mm(X("pK", 128 * j + k, 128 * j + 128, 16), X("dm", 2048 * j + k, 2048 * j + 2048, 16), X("g8"), False, k == 15)

    done = {0: 0, 1: 0, 2: 0, 3: 8}

    def fill(t, n):
        for _ in range(n):
            flush()
            if done[t] < 8:
                chunk(t, done[t])
                done[t] += 1

    def lists(c, offs, who, base, n):
        src = ind(X("morw", MO, 4624) if base else X("morw", MO, MD), X(offs, n * c // 16, n * c // 16 + n // 16))
        out = X("gd", n * c, n * c + n)
        if who == "s":
            act(out, src, AF.Copy)
        else:
            cp(out, src)

    flip = [0]

    def wide(c, dist, mv, n=1024):
        lo = (c % (2048 // n)) * n
        w = n // 16
        scan(X("es", lo, lo + n), X("rm", 0, n), X("gd", n * c, n * c + n), 0.0, OP.mult, OP.max)
        flip[0] ^= 1
        px = X("pX%d" % flip[0], 0, w)
        mm(px, X("idh"), X("es", lo + 15, lo + n, 16), True, False)
        mm(px, X("idn"), X(mv, w * c, w * c + w), False, True)
        act(X(dist, w * c, w * c + w), px, AF.Abs)

    def tl_a(par):
        tt(X("neq"), X("dri%d" % par, 0, 512), X("basi", par, 1024, 2), OP.not_equal)
        mm(X("pC"), X("tri"), X("neq"), True, True)
        act(X("sg"), X("pC"), AF.Sign, bias=X("thr"))
        act(X("pC"), X("sg"), AF.Copy, bias=2048.0, scale=2048.0)

    def tl_b(par):
        tt(X("tl", par, 1024, 2), X("pC"), X("dri%d" % par, 0, 512), OP.add)

    def z_tab(par):
        mm(X("pM"), X("wz"), X("mvt%d" % par, 0, 512), True, True)
        cp(X("kin", 0, 512), X("pM"))
        ts(X("kin", 0, 512), X("kin", 0, 512), 3, OP.bitwise_and)
        cp(X("junk"), X("kin", 0, 512))
        for b in range(16):
            mm(X("pU", 256, 288), X("dg", 128 * b, 128 * b + 128), X("junk", b, 512, 16), b == 0, b == 15)
        cp(X("zw%d" % par), X("pU", 256, 288))

    cp(X("mvt0", 0, 512), X("meas", 0, 1024, 2))
    for k in range(16):
        act(X("rep0", 4096 + k, 8192, 16), X("mvt0", 256, 512), AF.Copy)
    for c in range(2):
        cp(X("zsp", 0, 2048, 16), X("mvt0", 128 * c, 128 * c + 128))
        scan(X("rep0", 2048 * c, 2048 * c + 2048), X("rm"), X("zsp"), 0.0, OP.mult, OP.add)
    kap(0)
    prep(0)
    fill(0, 1)
    cp(X("dri0", 0, 512), X("deri", 0, 1024, 2))
    cp(X("dro0"), X("dri0", 0, 512))
    fill(0, 1)
    ms(X("bm"), -1.0)
    ms(X("one"), 1.0)
    ms(X("tri"), 1.0)
    ms(X("dri0", 512, 640), 0)
    ms(X("dri1", 512, 640), 0)
    ms(X("nd", 512, 640), 0)
    ms(X("mvt1", 512, 640), 0.0)
    cp(X("mvt1", 0, 512), X("meas", 1, 1024, 2))
    same(X("bm"), [], [[0, 16]])
    iota(X("tl", 1024, 2048), [[0, 1024]], 6144, 0, True)
    same(X("tri"), [], [[0, 16]])
    asel(X("tri"), [[1, 128]], OP.is_ge, 0, -1)
    for k in range(16):
        emit("g", lambda e: e.affine_select(T.rep1[:, k:8192:16], T.mvt1[:, 0:512], [[0, 512]], OP.is_ge, 0.0, 1, 0), [X("mvt1", 0, 512)],
             [X("rep1")] if k == 15 else [])

    def setup_0():
        ts(X("pk"), X("pi"), 15, OP.bitwise_and)
        ts(X("thr"), X("pk", 0, 1), 15, OP.is_ge, 1.5, OP.mult)
        ts(X("thr"), X("thr"), -0.5, OP.add)
        tl_a(0)
        cp(X("dri1", 0, 512), X("deri", 1, 1024, 2))
        ms(X("m8r"), 1.0)
        ms(X("m8r", 0, 256, 8), 0.0)

    def setup_1():
        cp(X("usef"), X("usei"))
        send(X("usef"), "uq0", 0, 1)
        tl_b(0)
        tl_a(1)

    def setup_a():
        for par in range(2):
            ts(X("bst%d" % par, 0, 512), X("basi", par, 1024, 2), 2048.0, OP.add)
            ms(X("bst%d" % par, 512, 640), 2048.0)
        ms(X("morw", MX, 4624), 16384.0)
        ms(X("marg"), 0.0)
        ms(X("on"), 1.0)
        tl_b(1)
        tt(X("iw"), X("pk"), X("i16"), OP.add)
        ts(X("bj"), X("iw", 0, 8), 0.5, OP.add)
        ts(X("j2"), X("iw", 0, 8), 2.0, OP.mult)
        send(X("tl", 0, 1024), "tq0", 0, 2)
        iota(X("xr"), [[2, 1024], [-1, 2]], 1, 0, True)
        iota(X("vr1"), [[2, 512]], 1, 0, True)
        iota(X("dg"), [[0, 2048]], 1, 0, True)
        asel(X("dg"), [[0, 16], [-16, 8], [-1, 16]], OP.is_equal, 0, 1)
        asel(X("dg"), [[-1, 16], [0, 8], [1, 16]], OP.is_equal, 0, 0)
        send(X("meas"), "mq1", 1, 3)
        send(X("meas"), "mq2", 2, 6)

    def setup_b():
        ms(X("gds", 512, 640), -100000.0)
        ms(X("got", 512, 640), 0.0)
        ms(X("cq", 512, 640), 0.0)
        ts(X("kin"), X("kin"), 15, OP.bitwise_and)
        ts(X("km"), X("kin"), 0, OP.is_equal)
        kap(1)
        kap(2)

    def setup_c():
        cp(X("dro1"), X("dri1", 0, 512))
        ts(X("jp"), X("pk", 0, 1), 1.0, OP.add)
        ts(X("wz"), X("b1"), X("jp"), OP.mult)
        z_tab(0)
        z_tab(1)

    for t in range(3):
        par = t % 2
        mvt, bst, dri = "mvt%d" % par, "bst%d" % par, "dri%d" % par
        for c in range(4):
            lists(c, "dro%d" % par, DSPLIT[t][c], 0, 2048)
            if t and c == 0:
                tl_a(1 - par)
            fill(t, DFILL[t][c] if c < 3 else 8)
            if t == 0 and c < 3:
                (setup_0, setup_1, setup_a)[c]()
            if t and c == 1:
                tl_b(1 - par)
                send(X("tl", 0, 1024), "tq%d" % t, t, 5 if t == 1 else 8)
            if 1 <= c < 3:
                wide(c - 1, "dd", mvt, 2048)
        flush()
        scan(X("ks"), X("minm"), X("pK"), BIG, OP.max, OP.min)
        for a in range(8):
            mm(X("pU", 32 * a, 32 * a + 32), X("la", 128 * a, 128 * a + 128), X("ks", 15, 512, 16), True, True)
        wide(2, "dd", mvt, 2048)
        tt(X("um"), X("pU", 0, 256), X("m8"), OP.mult)
        wide(3, "dd", mvt, 2048)
        mm(X("pD"), X("b1"), X("dd"), True, True)
        mm(X("pG"), X("bm"), X("dd"), True, False)
        scan(X("us"), X("m8r"), X("um"), 0.0, OP.mult, OP.add)
        mine = [c for c in range(8) if "G%d" % c not in EORD[t]]
        ahead = []

        def gather_e(n, top):
            for c in [c for c in mine if c not in ahead and c < top][:n]:
                lists(c, "eo", "s", 1, 1024)
                ahead.append(c)

        for h in range(2):
            for j in (2 * h, 2 * h + 1):
                cp(X("wi", 8 * j, 8 * j + 8), X("us", 8 * j + 7, 256, 32))
            w = (16 * h, 16 * h + 16)
            ts(X("wj", *w), X("wi", *w), 2047, OP.bitwise_and)
            cp(X("wo", *w), X("wj", *w))
            l = (256 * h, 256 * h + 256)
            tt(X("ec", *l), ind(X("tl"), X("wo", *w)), X(bst, *l), OP.max)
            ts(X("eo", *l), X("ec", *l), -2048.0, OP.add)
            if h == 0:
                gather_e(4, 4)
        if t == 0:
            setup_b()
        us = X("usef", 37 * t, 37 * t + 512)
        gather_e(4 - len(ahead), 8)
        for tok in EORD[t].split():
            c = int(tok[1])
            if tok[0] == "G":
                lists(c, "eo", "v", 1, 1024)
                continue
            gather_e(1, 8)
            wide(c, "ee", mvt)
            if c == 2:
                cp(X("dk"), ind(X("xr"), X("wo")))
            if c == 4:
                tt(X("pM"), X("dk"), us, OP.subtract)
                tt(X("dk"), X("pM"), X("km", t, t + 512), OP.mult)
        mm(X("pG"), X("b1"), X("ee"), False, True)
        ts(X("fail"), X("pG"), X("marg"), OP.add, 0.0, OP.is_ge)
        scan(X("cum"), X("fail"), X("fail"), 0.0, OP.add, OP.max)
        for a in range(8 - CNTV[t]):
            act(X("junk"), X("cum"), AF.Sign, bias=X("bj", a, a + 1), scale=-1.0, accum=X("acc", a, a + 1))
        act(X("cq", 0, 512), ind(X("uq%d" % t), X("kap%d" % t)), AF.Copy)
        act(X("gds", 0, 512), X("pD"), AF.Copy)
        act(X("got", 0, 512), X("fail"), AF.Copy, bias=1.0, scale=-1.0)
        mm(X("pC"), X("idn"), X("fail"), True, False)
        mm(X("pC"), X("idh"), X("one"), False, True)
        tt(X("pM"), X("dk"), X("pC"), OP.mult)
        tt(us, X("pM"), us, OP.add)
        if t < 2:
            send(X("usef"), "uq%d" % (t + 1), t + 1, 4 if t == 0 else 7)
            prep(t + 1)
        else:
            dma("y", T.yu[:], T.usef[:], R=[X("usef")])
        tt(X("pM"), X("ec"), X("pC"), OP.mult)
        tt(X("nd", 0, 512), X("pM"), X(dri, 0, 512), OP.max)
        for a in range(8 - CNTV[t], 8):
            ts(X("neq"), X("cum"), X("bj", a, a + 1), OP.is_le)
            red(X("acc", a, a + 1), X("neq"))
            ts(X("acc", a, a + 1), X("acc", a, a + 1), 2.0, OP.mult, -512.0, OP.add)
        if t == 0:
            setup_c()
        fill(t + 1, FILL[t][0])
        ts(X("sm"), X("acc"), 511.0, OP.is_gt)
        tt(X("sm"), X("sm"), X("j2"), OP.mult)
        tt(X("sm"), X("sm"), X("acc"), OP.add)
        ts(X("sel"), X("sm"), 0.5, OP.mult, 256.0, OP.add)
        cp(X("c2f"), ind(X("cq"), X("sel")))
        cp(X("c2o"), X("c2f"))
        cp(X("mv2"), ind(X(mvt), X("sel")))
        cp(X("zsp", 0, 2048, 16), X("mv2"))
        scan(X("rp2"), X("rm"), X("zsp"), 0.0, OP.mult, OP.add)
        mm(X("pC", 0, 128), X("c2f"), X("id1"), True, False)
        act(X("gd", 5120, 6144), ind(X("mq%d" % t), X("c2o", 64, 128)), AF.Copy)
        tt(X("gd", 4096, 5120), ind(X("mq%d" % t), X("c2o", 0, 64)), X("rp2", 0, 1024), OP.subtract)
        sub_abs("gd", 5120, "rp2", 1024)
        act(X("gd", 4096, 5120), X("gd", 4096, 5120), AF.Abs)
        for k in range(16):
            mm(X("pC", k, 128, 16), X("gd", 4096 + k, 6144, 16), X("g8"), False, k == 15)
        act(X("gd2"), ind(X("gds"), X("sel")), AF.Copy)
        cp(X("bs2"), ind(X(bst), X("sel")))
        cp(X("dr2"), ind(X(dri), X("sel")))
        fill(t + 1, FILL[t][1])
        scan(X("ks2"), X("minm", 0, 128), X("pC", 0, 128), BIG, OP.max, OP.min)
        for a in range(8):
            mm(X("pU", 8 * a, 8 * a + 8), X("la", 128 * a, 128 * a + 128), X("ks2", 15, 128, 16), True, True)
        fill(t + 1, FILL[t][2])
        tt(X("um2"), X("pU", 0, 64), X("m8", 0, 64), OP.mult)
        scan(X("us2"), X("m8r", 0, 64), X("um2"), 0.0, OP.mult, OP.add)
        cp(X("wi", 0, 8), X("us2", 7, 64, 8))
        ts(X("wj", 0, 8), X("wi", 0, 8), 2047, OP.bitwise_and)
        cp(X("w2o"), X("wj", 0, 8))
        tt(X("ec2"), ind(X("tq%d" % t), X("w2o")), X("bs2"), OP.max)
        ts(X("eo2"), X("ec2"), -2048.0, OP.add)
        lists(0, "eo2", "s", 1, 1024)
        lists(1, "eo2", "v", 1, 1024)
        wide(0, "ee2", "mv2")
        wide(1, "ee2", "mv2")
        mm(X("pD", 0, 128), X("b1"), X("ee2"), True, True)
        cp(X("zi"), X("zw%d" % par))
        ts(X("zt"), X("zi"), t, OP.add)
        ts(X("zu"), X("zt"), 3, OP.bitwise_and)
        ts(X("zc"), X("iw"), 3.0, OP.mult, float(MO), OP.add)
        tt(X("zc"), X("zc"), X("zu"), OP.add)
        fill(t + 1, FILL[t][3])
        tt(X("x2"), X("pD", 0, 128), X("gd2"), OP.subtract)
        ts(X("ad2"), X("x2"), X("marg"), OP.add, 0.0, OP.is_lt)
        cp(ind(X("got"), X("sel")), X("ad2"))
        for b in range(16):
            mm(X("pU", 256, 288), X("dg", 128 * b, 128 * b + 128), X("got", b, 512, 16), b == 0, b == 15)
        tt(X("y2"), X("ad2"), X("ec2"), OP.mult)
        tt(X("n2"), X("y2"), X("dr2"), OP.max)
        tt(X("gf"), X("pU", 256, 288), X("zc"), OP.mult)
        tt(X("gf"), X("gf"), X("iw"), OP.add)
        cp(X("gu"), X("gf"))
        cp(ind(X("morw", 0, MD), X("gu")), X(mvt, 0, 512))
        if t < 2:
            red(X("cn"), X("pU", 256, 288))
            mm(X("pC", 0, 1), X("on"), X("cn"), True, True)
            dma("y", T.morw[:, MD:MX], T.morw[:, MO:MD], R=[X("morw", MO, MD)], W=[X("morw", MD, MX)])
        else:
            dma("s", T.ym[:], T.morw[:, MO:MD], R=[X("morw", MO, MD)])
        cp(ind(X("nd"), X("sel")), X("n2"))
        ts(X(dri), X("nd"), 2047, OP.bitwise_and)
        if t < 2:
            cp(X("wi", 0, 1), X("pC", 0, 1))
            ts(X("wj", 0, 1), X("wi", 0, 1), 127, OP.bitwise_and)
            cp(X("marg"), X("wj", 0, 1))
            if t == 0:
                cp(X("dro0"), X("dri0", 0, 512))
        if t > 0:
            cp(X("ydb", par, 1024, 2), X(dri, 0, 512))
    dma("y", T.yd[:], T.ydb[:], R=[X("ydb")])
    for s in sorted(total):
        if clock["g"].get(s, 0) < total[s]:
            g.wait_ge(T.sem[s], total[s])
